import numpy as np
import ml_dtypes


def mxq(x, axis, fmt="e4m3"):
    dtype, down = {"e4m3": (ml_dtypes.float8_e4m3fn, 7), "e5m2": (ml_dtypes.float8_e5m2, 14)}[fmt]
    v = np.moveaxis(np.asarray(x, np.float32).astype(ml_dtypes.bfloat16).astype(np.float64), axis, -1)
    blocks = v.reshape(v.shape[:-1] + (-1, 32))
    amax = np.abs(blocks).max(-1, keepdims=True)
    byte = np.maximum(np.where(amax > 0, np.frexp(amax)[1] - 1 + 127, 0) - down, 1)
    scale = np.exp2(byte - 127.0)
    codes = (blocks / scale).astype(np.float32).astype(dtype).astype(np.float64)
    return np.moveaxis((codes * scale).reshape(v.shape), -1, axis)


WIDE = False


def mx_kscale(k):
    if not WIDE:
        return np.ones(k)
    levels = np.array([10, -10, 5, -5, 0])
    if k % 512:
        return np.exp2(np.random.permutation(np.resize(levels, k // 32))).repeat(32)
    a = np.empty((k // 512, 16))
    for p in range(k // 512):
        a[p, :8] = np.random.permutation(np.resize(levels, 8))
        for g in range(8):
            far = levels[np.abs(levels - a[p, g]) >= 10]
            a[p, g + 8] = far[np.random.randint(len(far))]
    return np.exp2(a.ravel()).repeat(32)


def f64(x):
    return np.asarray(x).astype(np.float64)


def striped(idx):
    return np.tile(idx.reshape(-1, 16).T, (8, 1)).astype(np.uint16)


def unstriped(offs):
    return offs[:16].T.reshape(-1).astype(np.int64)


E2M1 = np.array([0.0, 0.5, 1.0, 1.5, 2.0, 3.0, 4.0, 6.0, -0.0, -0.5, -1.0, -1.5, -2.0, -3.0, -4.0, -6.0])


def pack_weight(w, fmt):
    k, n = w.shape
    w = f64(np.asarray(w, np.float32).astype(ml_dtypes.bfloat16)).reshape(k // 32, 32, n)
    amax = np.abs(w).max(1)
    if fmt == "e4m3":
        byte = np.frexp(amax)[1] - 1 + 127 - 7
    else:
        mant, ex = np.frexp(amax / 6.0)
        byte = np.where(mant > 0.5, ex, ex - 1) + 127
    byte = np.clip(np.where(amax > 0, byte, 1), 1, 254)
    scaled = (w * np.exp2(127.0 - byte)[:, None, :]).reshape(k, n).astype(np.float32)
    by_word = np.ascontiguousarray(scaled.reshape(k // 512, 128, 4, n).transpose(0, 1, 3, 2))
    if fmt == "e4m3":
        words = by_word.astype(ml_dtypes.float8_e4m3fn).view(np.uint8)
    else:
        c = by_word.astype(ml_dtypes.float4_e2m1fn).view(np.uint8) & 0xF
        words = (c[..., 0::2] | (c[..., 1::2] << 4)).reshape(k // 512, 128, 2 * n)
    return np.ascontiguousarray(words), np.ascontiguousarray(byte.astype(np.uint8).reshape(k // 512, 16, n))


def unpack_weight(words, scales, fmt):
    g, _, n = scales.shape
    words = np.ascontiguousarray(words).reshape(g, 128, n, -1)
    if fmt == "e4m3":
        vals = words.view(ml_dtypes.float8_e4m3fn).astype(np.float64)
    else:
        nib = np.empty((g, 128, n, 4), np.uint8)
        nib[..., 0::2] = words & 0xF
        nib[..., 1::2] = words >> 4
        vals = E2M1[nib]
    vals = vals * np.repeat(np.exp2(scales.astype(np.float64) - 127.0), 8, axis=1)[..., None]
    return vals.transpose(0, 1, 3, 2).reshape(g * 512, n)


K, T, E, N = 1024, 2048, 8, 128
COUNTS = (128, 128, 128, 256, 128, 384, 384, 512)
STARTS = np.cumsum((0,) + COUNTS)
K8 = 512


def by_expert(wq, xq):
    return np.concatenate([wq[e].T @ xq[:, STARTS[e]:STARTS[e + 1]] for e in range(E)], axis=1)


def setup_inputs():
    n = np.random.standard_normal
    s = mx_kscale(K)[:, None]
    expert = np.random.permutation(np.repeat(np.arange(E), COUNTS))
    slot_token = np.argsort(expert, kind="stable")
    w = n((E, K, N)) / np.sqrt(K) / s[None]
    w8 = [pack_weight(m[:K8], "e4m3") for m in w]
    w4 = [pack_weight(m[K8:], "e2m1") for m in w]
    return {
        "xT": (n((K, T)) * s).astype(np.float32),
        "w8_words": np.stack([m[0] for m in w8]),
        "w8_scales": np.stack([m[1] for m in w8]),
        "w4_words": np.stack([m[0] for m in w4]),
        "w4_scales": np.stack([m[1] for m in w4]),
        "b": (0.3 * n((N, E))).astype(np.float32),
        "gate": np.tile(np.random.uniform(0.2, 1.0, T), (N, 1)).astype(np.float32),
        "offs": striped(slot_token),
    }


def reference(xT, w8_words, w8_scales, w4_words, w4_scales, b, gate, offs):
    idx = unstriped(offs)
    w = np.stack([np.concatenate([unpack_weight(w8_words[e], w8_scales[e], "e4m3"), unpack_weight(w4_words[e], w4_scales[e], "e2m1")]) for e in range(E)])
    xq = mxq(f64(xT)[:, idx], 0, "e4m3")
    y = by_expert(w, xq)
    y = y + np.repeat(f64(b), COUNTS, axis=1)
    out = np.zeros((N, T))
    out[:, idx] = f64(gate) * y
    return out

@@ -1,0 +1,164 @@
+from contextlib import ExitStack
+
+import concourse.mybir as mybir
+
+K, T, E, N = 1024, 2048, 8, 128
+COUNTS = (128, 128, 128, 256, 128, 384, 384, 512)
+STARTS = tuple(sum(COUNTS[:e]) for e in range(E + 1))
+FLOPS = 2 * T * K * N
+
+P = 128
+PACK = 4
+BANK = 512
+
+F32 = mybir.dt.float32
+BF16 = mybir.dt.bfloat16
+I32 = mybir.dt.int32
+U32 = mybir.dt.uint32
+U16 = mybir.dt.uint16
+U8 = mybir.dt.uint8
+FP8X4 = mybir.dt.float8_e4m3fn_x4
+FP4X4 = mybir.dt.float4_e2m1fn_x4
+COPY = mybir.ActivationFunctionType.Copy
+IDENTITY = mybir.ActivationFunctionType.Identity
+MULT = mybir.AluOpType.mult
+
+CHUNKS = (
+    ((256, 96), (256, 128), (512, 256), (512, 256), (256, 144), (256, 176)),
+    ((512, 64), (512, 96), (512, 112), (256, 80), (256, 160)),
+)
+QCOLS = 512
+PIECES = ((0, 640), (640, 1536), (1536, 2048))
+EARLY = ((0, 768), (768, 1536), (1536, 2048))
+
+
+def tile_moe_rag_lin_bias_kernel(
+    tc, xT, w8_words, w8_scales, w4_words, w4_scales, b, gate, offs, out
+):
+    nc = tc.nc
+    with ExitStack() as ctx:
+        keep = ctx.enter_context(tc.tile_pool(name="keep", bufs=1))
+        psum = ctx.enter_context(tc.psum_pool(name="psum", bufs=1))
+
+        offsets = keep.tile([P, T // 16], U16, name="offsets")
+        w8 = keep.tile([P, E * N * 4], U8, name="w8", align_bytes=64)
+        w4 = keep.tile([P, E * N * 2], U8, name="w4", align_bytes=64)
+        wsc = keep.tile([P, E * N], U8, name="wsc", align_bytes=64)
+        bias = keep.tile([P, E], F32, name="bias")
+        gates = keep.tile([P, T], F32, name="gates")
+        sc = keep.tile([P, T], U8, name="sc", align_bytes=64)
+        gsc = keep.tile([P, T], U8, name="gsc", align_bytes=64)
+        words = [keep.tile([P, T], U32, name=f"words{g}", align_bytes=64) for g in range(2)]
+        gwords = [keep.tile([P, T], U32, name=f"gwords{g}", align_bytes=64) for g in range(2)]
+        xb = [keep.tile([P, T * PACK], BF16, name=f"xb{g}", align_bytes=64) for g in range(2)]
+        y = keep.tile([P, T], F32, name="y")
+        win = keep.tile([P, T], F32, name="win")
+        banks = [psum.tile([P, BANK], F32, name=f"bank{i}") for i in range(E)]
+
+        nc.vector.memset(wsc[:].bitcast(I32), 0)
+        nc.vector.memset(sc[:].bitcast(I32), 0)
+        wsc_i = wsc[:].bitcast(I32).rearrange("p (e n) -> p e n", e=E)
+
+        def load_scales(n):
+            q = n % 4
+            source = (w4_scales, w8_scales)[n // 4]
+            src = source[:, 0, 4 * q : 4 * q + 4, :].rearrange("e q n -> q e n").bitcast(I32)
+            start = 32 * q + n // 4 * 4
+            nc.sync.dma_start(wsc_i[start : start + 4], src)
+
+        scale_order = {(0, 3): (0, 1), (0, 4): (2, 3), (1, 0): (4, 5), (1, 1): (6, 7)}
+
+        def load_words():
+            nc.sync.dma_start(
+                w4[:].bitcast(I32).rearrange("p (e n) -> p e n", e=E),
+                w4_words.rearrange("e a p n -> p (e a) n").bitcast(I32),
+            )
+            nc.sync.dma_start(
+                w8[:].bitcast(I32).rearrange("p (e n) -> p e n", e=E),
+                w8_words.rearrange("e a p n r -> p (e a) (n r)").bitcast(I32),
+            )
+
+        raw = []
+        for g in range(2):
+            rows = xT[512 * g : 512 * g + 512, :].rearrange("(p j) w -> p j w", j=PACK)
+            c0 = 0
+            for n, (width, share) in enumerate(CHUNKS[g]):
+                r = keep.tile([P, PACK, width], F32, name=f"raw{g}_{n}")
+                nc.sync.dma_start(r[:], rows[:, :, c0 : c0 + width])
+                raw.append((g, c0, width, share, r))
+                c0 += width
+                if g == 0 and n == 0:
+                    nc.sync.dma_start(offsets[:], offs)
+                    nc.sync.dma_start(bias[:], b)
+                for m in scale_order.get((g, n), ()):
+                    load_scales(m)
+        load_words()
+        nc.sync.dma_start(gates[:], gate)
+
+        def round_part(engine, g, c0, r, lo, hi):
+            dst = xb[g][:, (c0 + lo) * PACK : (c0 + hi) * PACK].rearrange("p (c i t) -> p c t i", i=4, t=PACK)
+            src = r[:, :, lo:hi].rearrange("p t (c i) -> p c t i", i=4)
+            if engine == 0:
+                nc.vector.tensor_copy(dst, src)
+            else:
+                nc.scalar.activation(dst, src, COPY)
+
+        def quantize(g, c0, width):
+            step = min(width, QCOLS)
+            for q in range(c0, c0 + width, step):
+                cols = slice(q, q + step)
+                nc.vector.quantize_mx(
+                    out=words[g][:, cols].bitcast(FP8X4),
+                    scales=sc[4:, cols] if g == 0 else sc[:, cols],
+                    in_=xb[g][:, q * PACK : (q + step) * PACK],
+                )
+
+        def gather_words(g, lo, hi):
+            nc.vector.tensor_copy(gwords[g][:, lo:hi], words[g][:].indirect(offsets[:, lo // 16 : hi // 16]))
+
+        def gather_scales(lo, hi):
+            nc.vector.tensor_copy(gsc[:, lo:hi], sc[:].indirect(offsets[:, lo // 16 : hi // 16]))
+
+        early = list(EARLY)
+        for g, c0, width, share, r in raw:
+            round_part(0, g, c0, r, 0, share)
+            round_part(1, g, c0, r, share, width)
+            if g == 1 and early:
+                gather_words(0, *early.pop(0))
+            quantize(g, c0, width)
+
+        def expert(e):
+            slots = slice(STARTS[e], STARTS[e + 1])
+            w4_e = w4[:, e * N * 2 : (e + 1) * N * 2].bitcast(FP4X4)
+            w8_e = w8[:, e * N * 4 : (e + 1) * N * 4].bitcast(FP8X4)
+            step = BANK if COUNTS[e] == BANK else 128
+            for c in range(0, COUNTS[e], step):
+                cols = slice(STARTS[e] + c, STARTS[e] + c + step)
+                acc = banks[e][:, c : c + step]
+                nc.tensor.matmul_mx(
+                    out=acc, lhsT=w8_e, lhsT_scale=wsc[4:, e * N : (e + 1) * N],
+                    rhs=gwords[0][:, cols].bitcast(FP8X4), rhs_scale=gsc[4:, cols],
+                    start=True, stop=False,
+                )
+                nc.tensor.matmul_mx(
+                    out=acc, lhsT=w4_e, lhsT_scale=wsc[:, e * N : (e + 1) * N],
+                    rhs=gwords[1][:, cols].bitcast(FP8X4), rhs_scale=gsc[:, cols],
+                    start=False, stop=True,
+                )
+            nc.scalar.activation(y[:, slots], banks[e][:, : COUNTS[e]], IDENTITY, bias=bias[:, e : e + 1])
+
+        def scatter(lo, hi):
+            nc.vector.tensor_tensor(
+                win[:].indirect(offsets[:, lo // 16 : hi // 16]), y[:, lo:hi], gates[:, lo:hi], MULT
+            )
+
+        for i, (lo, hi) in enumerate(PIECES):
+            gather_words(1, lo, hi)
+            gather_scales(lo, hi)
+            for e in range(E):
+                if lo <= STARTS[e] < hi:
+                    expert(e)
+            if i:
+                scatter(*PIECES[i - 1])
+        scatter(*PIECES[-1])
+        nc.sync.dma_start(out, win[:])

@@ -24,8 +24,8 @@ IDENTITY = mybir.ActivationFunctionType.Identity
 MULT = mybir.AluOpType.mult
 
 CHUNKS = (
-    ((256, 96), (256, 128), (512, 256), (512, 256), (256, 144), (256, 176)),
-    ((512, 64), (512, 96), (512, 112), (256, 80), (256, 160)),
+    ((1024, 576), (512, 224), (512, 272)),
+    ((512, 96), (512, 96), (512, 112), (256, 80), (256, 160)),
 )
 QCOLS = 512
 PIECES = ((0, 640), (640, 1536), (1536, 2048))
@@ -59,14 +59,16 @@ def tile_moe_rag_lin_bias_kernel(
         nc.vector.memset(sc[:].bitcast(I32), 0)
         wsc_i = wsc[:].bitcast(I32).rearrange("p (e n) -> p e n", e=E)
 
-        def load_scales(n):
+        def load_scales(engine, n):
             q = n % 4
             source = (w4_scales, w8_scales)[n // 4]
             src = source[:, 0, 4 * q : 4 * q + 4, :].rearrange("e q n -> q e n").bitcast(I32)
             start = 32 * q + n // 4 * 4
-            nc.sync.dma_start(wsc_i[start : start + 4], src)
+            engine.dma_start(wsc_i[start : start + 4], src)
 
-        scale_order = {(0, 3): (0, 1), (0, 4): (2, 3), (1, 0): (4, 5), (1, 1): (6, 7)}
+        for n in range(4):
+            load_scales(nc.scalar, n)
+
 
         def load_words():
             nc.sync.dma_start(
@@ -89,11 +91,13 @@ def tile_moe_rag_lin_bias_kernel(
                 c0 += width
                 if g == 0 and n == 0:
                     nc.sync.dma_start(offsets[:], offs)
+                if g == 1 and n == 0:
                     nc.sync.dma_start(bias[:], b)
-                for m in scale_order.get((g, n), ()):
-                    load_scales(m)
         load_words()
-        nc.sync.dma_start(gates[:], gate)
+        for n in range(4, 8):
+            load_scales(nc.sync, n)
+        for c0 in (0, T // 2):
+            nc.sync.dma_start(gates[:, c0 : c0 + T // 2], gate[:, c0 : c0 + T // 2])
 
         def round_part(engine, g, c0, r, lo, hi):
             dst = xb[g][:, (c0 + lo) * PACK : (c0 + hi) * PACK].rearrange("p (c i t) -> p c t i", i=4, t=PACK)

@@ -28,7 +28,8 @@ CHUNKS = (
     ((512, 96), (512, 96), (512, 112), (256, 80), (256, 160)),
 )
 QCOLS = 512
-PIECES = ((0, 640), (640, 1536), (1536, 2048))
+PIECES = ((0, 768), (768, 1536), (1536, 2048))
+SCATTERS = ((0, 768), (768, 2048))
 EARLY = ((0, 768), (768, 1536), (1536, 2048))
 
 
@@ -52,6 +53,7 @@ def tile_moe_rag_lin_bias_kernel(
         gwords = [keep.tile([P, T], U32, name=f"gwords{g}", align_bytes=64) for g in range(2)]
         xb = [keep.tile([P, T * PACK], BF16, name=f"xb{g}", align_bytes=64) for g in range(2)]
         y = keep.tile([P, T], F32, name="y")
+        z = keep.tile([P, T], F32, name="z")
         win = keep.tile([P, T], F32, name="win")
         banks = [psum.tile([P, BANK], F32, name=f"bank{i}") for i in range(E)]
 
@@ -68,6 +70,7 @@ def tile_moe_rag_lin_bias_kernel(
 
         for n in range(4):
             load_scales(nc.scalar, n)
+            load_scales(nc.gpsimd, 4 + n)
 
 
         def load_words():
@@ -94,8 +97,6 @@ def tile_moe_rag_lin_bias_kernel(
                 if g == 1 and n == 0:
                     nc.sync.dma_start(bias[:], b)
         load_words()
-        for n in range(4, 8):
-            load_scales(nc.sync, n)
         for c0 in (0, T // 2):
             nc.sync.dma_start(gates[:, c0 : c0 + T // 2], gate[:, c0 : c0 + T // 2])
 
@@ -151,18 +152,19 @@ def tile_moe_rag_lin_bias_kernel(
                 )
             nc.scalar.activation(y[:, slots], banks[e][:, : COUNTS[e]], IDENTITY, bias=bias[:, e : e + 1])
 
-        def scatter(lo, hi):
-            nc.vector.tensor_tensor(
-                win[:].indirect(offsets[:, lo // 16 : hi // 16]), y[:, lo:hi], gates[:, lo:hi], MULT
-            )
+        def weigh(lo, hi):
+            nc.gpsimd.tensor_tensor(z[:, lo:hi], y[:, lo:hi], gates[:, lo:hi], MULT)
 
-        for i, (lo, hi) in enumerate(PIECES):
+        for lo, hi in PIECES:
             gather_words(1, lo, hi)
             gather_scales(lo, hi)
+            first = lo
             for e in range(E):
                 if lo <= STARTS[e] < hi:
                     expert(e)
-            if i:
-                scatter(*PIECES[i - 1])
-        scatter(*PIECES[-1])
+                    if STARTS[e + 1] - first >= 384:
+                        weigh(first, STARTS[e + 1])
+                        first = STARTS[e + 1]
+        for lo, hi in SCATTERS:
+            nc.vector.tensor_copy(win[:].indirect(offsets[:, lo // 16 : hi // 16]), z[:, lo:hi])
         nc.sync.dma_start(out, win[:])

@@ -28,8 +28,8 @@ CHUNKS = (
     ((512, 96), (512, 96), (512, 112), (256, 80), (256, 160)),
 )
 QCOLS = 512
-PIECES = ((0, 768), (768, 1536), (1536, 2048))
-SCATTERS = ((0, 768), (768, 2048))
+PIECES = ((0, 1024), (1024, 2048))
+SCATTERS = ((0, 768), (768, 1536), (1536, 2048))
 EARLY = ((0, 768), (768, 1536), (1536, 2048))
 
 
@@ -53,7 +53,6 @@ def tile_moe_rag_lin_bias_kernel(
         gwords = [keep.tile([P, T], U32, name=f"gwords{g}", align_bytes=64) for g in range(2)]
         xb = [keep.tile([P, T * PACK], BF16, name=f"xb{g}", align_bytes=64) for g in range(2)]
         y = keep.tile([P, T], F32, name="y")
-        z = keep.tile([P, T], F32, name="z")
         win = keep.tile([P, T], F32, name="win")
         banks = [psum.tile([P, BANK], F32, name=f"bank{i}") for i in range(E)]
 
@@ -68,20 +67,6 @@ def tile_moe_rag_lin_bias_kernel(
             start = 32 * q + n // 4 * 4
             engine.dma_start(wsc_i[start : start + 4], src)
 
-        for n in range(4):
-            load_scales(nc.scalar, n)
-            load_scales(nc.gpsimd, 4 + n)
-
-
-        def load_words():
-            nc.sync.dma_start(
-                w4[:].bitcast(I32).rearrange("p (e n) -> p e n", e=E),
-                w4_words.rearrange("e a p n -> p (e a) n").bitcast(I32),
-            )
-            nc.sync.dma_start(
-                w8[:].bitcast(I32).rearrange("p (e n) -> p e n", e=E),
-                w8_words.rearrange("e a p n r -> p (e a) (n r)").bitcast(I32),
-            )
 
         raw = []
         for g in range(2):
@@ -94,9 +79,19 @@ def tile_moe_rag_lin_bias_kernel(
                 c0 += width
                 if g == 0 and n == 0:
                     nc.sync.dma_start(offsets[:], offs)
-                if g == 1 and n == 0:
-                    nc.sync.dma_start(bias[:], b)
-        load_words()
+        nc.sync.dma_start(
+            w4[:].bitcast(I32).rearrange("p (e n) -> p e n", e=E),
+            w4_words.rearrange("e a p n -> p (e a) n").bitcast(I32),
+        )
+        for n in range(6):
+            load_scales(nc.sync, n)
+        nc.sync.dma_start(
+            w8[:].bitcast(I32).rearrange("p (e n) -> p e n", e=E),
+            w8_words.rearrange("e a p n r -> p (e a) (n r)").bitcast(I32),
+        )
+        for n in range(6, 8):
+            load_scales(nc.sync, n)
+        nc.sync.dma_start(bias[:], b)
         for c0 in (0, T // 2):
             nc.sync.dma_start(gates[:, c0 : c0 + T // 2], gate[:, c0 : c0 + T // 2])
 
@@ -152,19 +147,16 @@ def tile_moe_rag_lin_bias_kernel(
                 )
             nc.scalar.activation(y[:, slots], banks[e][:, : COUNTS[e]], IDENTITY, bias=bias[:, e : e + 1])
 
-        def weigh(lo, hi):
-            nc.gpsimd.tensor_tensor(z[:, lo:hi], y[:, lo:hi], gates[:, lo:hi], MULT)
+        def scatter(lo, hi):
+            nc.vector.tensor_tensor(
+                win[:].indirect(offsets[:, lo // 16 : hi // 16]), y[:, lo:hi], gates[:, lo:hi], MULT
+            )
 
         for lo, hi in PIECES:
             gather_words(1, lo, hi)
             gather_scales(lo, hi)
-            first = lo
-            for e in range(E):
-                if lo <= STARTS[e] < hi:
-                    expert(e)
-                    if STARTS[e + 1] - first >= 384:
-                        weigh(first, STARTS[e + 1])
-                        first = STARTS[e + 1]
+        for e in range(E):
+            expert(e)
         for lo, hi in SCATTERS:
-            nc.vector.tensor_copy(win[:].indirect(offsets[:, lo // 16 : hi // 16]), z[:, lo:hi])
+            scatter(lo, hi)
         nc.sync.dma_start(out, win[:])

from contextlib import ExitStack

import concourse.mybir as mybir

K, T, E, N = 1024, 2048, 8, 128
COUNTS = (128, 128, 128, 256, 128, 384, 384, 512)
STARTS = tuple(sum(COUNTS[:e]) for e in range(E + 1))
FLOPS = 2 * T * K * N

P = 128
PACK = 4
BANK = 512

F32 = mybir.dt.float32
BF16 = mybir.dt.bfloat16
I32 = mybir.dt.int32
U32 = mybir.dt.uint32
U16 = mybir.dt.uint16
U8 = mybir.dt.uint8
FP8X4 = mybir.dt.float8_e4m3fn_x4
FP4X4 = mybir.dt.float4_e2m1fn_x4
COPY = mybir.ActivationFunctionType.Copy
IDENTITY = mybir.ActivationFunctionType.Identity
MULT = mybir.AluOpType.mult

CHUNKS = (
    ((1024, 576), (512, 224), (512, 272)),
    ((512, 96), (512, 96), (512, 112), (256, 80), (256, 160)),
)
QCOLS = 512
PIECES = ((0, 1024), (1024, 2048))
SCATTERS = ((0, 768), (768, 1536), (1536, 2048))
EARLY = ((0, 768), (768, 1536), (1536, 2048))


def tile_moe_rag_lin_bias_kernel(
    tc, xT, w8_words, w8_scales, w4_words, w4_scales, b, gate, offs, out
):
    nc = tc.nc
    with ExitStack() as ctx:
        keep = ctx.enter_context(tc.tile_pool(name="keep", bufs=1))
        psum = ctx.enter_context(tc.psum_pool(name="psum", bufs=1))

        offsets = keep.tile([P, T // 16], U16, name="offsets")
        w8 = keep.tile([P, E * N * 4], U8, name="w8", align_bytes=64)
        w4 = keep.tile([P, E * N * 2], U8, name="w4", align_bytes=64)
        wsc = keep.tile([P, E * N], U8, name="wsc", align_bytes=64)
        bias = keep.tile([P, E], F32, name="bias")
        gates = keep.tile([P, T], F32, name="gates")
        sc = keep.tile([P, T], U8, name="sc", align_bytes=64)
        gsc = keep.tile([P, T], U8, name="gsc", align_bytes=64)
        words = [keep.tile([P, T], U32, name=f"words{g}", align_bytes=64) for g in range(2)]
        gwords = [keep.tile([P, T], U32, name=f"gwords{g}", align_bytes=64) for g in range(2)]
        xb = [keep.tile([P, T * PACK], BF16, name=f"xb{g}", align_bytes=64) for g in range(2)]
        y = keep.tile([P, T], F32, name="y")
        win = keep.tile([P, T], F32, name="win")
        banks = [psum.tile([P, BANK], F32, name=f"bank{i}") for i in range(E)]

        nc.vector.memset(wsc[:].bitcast(I32), 0)
        nc.vector.memset(sc[:].bitcast(I32), 0)
        wsc_i = wsc[:].bitcast(I32).rearrange("p (e n) -> p e n", e=E)

        def load_scales(engine, n):
            q = n % 4
            source = (w4_scales, w8_scales)[n // 4]
            src = source[:, 0, 4 * q : 4 * q + 4, :].rearrange("e q n -> q e n").bitcast(I32)
            start = 32 * q + n // 4 * 4
            engine.dma_start(wsc_i[start : start + 4], src)


        raw = []
        for g in range(2):
            rows = xT[512 * g : 512 * g + 512, :].rearrange("(p j) w -> p j w", j=PACK)
            c0 = 0
            for n, (width, share) in enumerate(CHUNKS[g]):
                r = keep.tile([P, PACK, width], F32, name=f"raw{g}_{n}")
                nc.sync.dma_start(r[:], rows[:, :, c0 : c0 + width])
                raw.append((g, c0, width, share, r))
                c0 += width
                if g == 0 and n == 0:
                    nc.sync.dma_start(offsets[:], offs)
        nc.sync.dma_start(
            w4[:].bitcast(I32).rearrange("p (e n) -> p e n", e=E),
            w4_words.rearrange("e a p n -> p (e a) n").bitcast(I32),
        )
        for n in range(6):
            load_scales(nc.sync, n)
        nc.sync.dma_start(
            w8[:].bitcast(I32).rearrange("p (e n) -> p e n", e=E),
            w8_words.rearrange("e a p n r -> p (e a) (n r)").bitcast(I32),
        )
        for n in range(6, 8):
            load_scales(nc.sync, n)
        nc.sync.dma_start(bias[:], b)
        for c0 in (0, T // 2):
            nc.sync.dma_start(gates[:, c0 : c0 + T // 2], gate[:, c0 : c0 + T // 2])

        def round_part(engine, g, c0, r, lo, hi):
            dst = xb[g][:, (c0 + lo) * PACK : (c0 + hi) * PACK].rearrange("p (c i t) -> p c t i", i=4, t=PACK)
            src = r[:, :, lo:hi].rearrange("p t (c i) -> p c t i", i=4)
            if engine == 0:
                nc.vector.tensor_copy(dst, src)
            else:
                nc.scalar.activation(dst, src, COPY)

        def quantize(g, c0, width):
            step = min(width, QCOLS)
            for q in range(c0, c0 + width, step):
                cols = slice(q, q + step)
                nc.vector.quantize_mx(
                    out=words[g][:, cols].bitcast(FP8X4),
                    scales=sc[4:, cols] if g == 0 else sc[:, cols],
                    in_=xb[g][:, q * PACK : (q + step) * PACK],
                )

        def gather_words(g, lo, hi):
            nc.vector.tensor_copy(gwords[g][:, lo:hi], words[g][:].indirect(offsets[:, lo // 16 : hi // 16]))

        def gather_scales(lo, hi):
            nc.vector.tensor_copy(gsc[:, lo:hi], sc[:].indirect(offsets[:, lo // 16 : hi // 16]))

        early = list(EARLY)
        for g, c0, width, share, r in raw:
            round_part(0, g, c0, r, 0, share)
            round_part(1, g, c0, r, share, width)
            if g == 1 and early:
                gather_words(0, *early.pop(0))
            quantize(g, c0, width)

        def expert(e):
            slots = slice(STARTS[e], STARTS[e + 1])
            w4_e = w4[:, e * N * 2 : (e + 1) * N * 2].bitcast(FP4X4)
            w8_e = w8[:, e * N * 4 : (e + 1) * N * 4].bitcast(FP8X4)
            step = BANK if COUNTS[e] == BANK else 128
            for c in range(0, COUNTS[e], step):
                cols = slice(STARTS[e] + c, STARTS[e] + c + step)
                acc = banks[e][:, c : c + step]
                nc.tensor.matmul_mx(
                    out=acc, lhsT=w8_e, lhsT_scale=wsc[4:, e * N : (e + 1) * N],
                    rhs=gwords[0][:, cols].bitcast(FP8X4), rhs_scale=gsc[4:, cols],
                    start=True, stop=False,
                )
                nc.tensor.matmul_mx(
                    out=acc, lhsT=w4_e, lhsT_scale=wsc[:, e * N : (e + 1) * N],
                    rhs=gwords[1][:, cols].bitcast(FP8X4), rhs_scale=gsc[:, cols],
                    start=False, stop=True,
                )
            nc.scalar.activation(y[:, slots], banks[e][:, : COUNTS[e]], IDENTITY, bias=bias[:, e : e + 1])

        def scatter(lo, hi):
            nc.vector.tensor_tensor(
                win[:].indirect(offsets[:, lo // 16 : hi // 16]), y[:, lo:hi], gates[:, lo:hi], MULT
            )

        for lo, hi in PIECES:
            gather_words(1, lo, hi)
            gather_scales(lo, hi)
        for e in range(E):
            expert(e)
        for lo, hi in SCATTERS:
            scatter(lo, hi)
        nc.sync.dma_start(out, win[:])
